import numpy as np, ml_dtypes
CORES = [48,49,50,51,52,53,54,55,72,73,74,75,76,77,78,79]
N = 16
GROUPS = [[0,1,2,3,4,5,6,7],[8,9,10,11,12,13,14,15]]
def setup_inputs(rng):
    return {"x": rng.standard_normal((N, 128, 8), dtype=np.float32).astype(ml_dtypes.bfloat16)}
def reference(x):
    y = np.empty((N, 128, 64), x.dtype)
    for g in GROUPS:
        s = np.concatenate([x[r] for r in g], axis=1)
        for r in g:
            y[r] = s
    return {"y": y}

from concourse.bass import DstId, RemoteDMATransfer

SCRATCH = {
    "stage": ("dram", [128, 8], "bfloat16"),
    "land": ("sbuf", [128, 64], "bfloat16"),
}
SEMAPHORES = ["staged", "sent", "arrived", "stored"]


def rank_program(g, core, T, topo):
    rank = T.rank_of(core)
    if rank is None:
        return
    group = [grp for grp in T.tables["GROUPS"] if rank in grp][0]
    pos = group.index(rank)
    w = T.x.shape[1]
    mine = T.land[:, pos * w:(pos + 1) * w]
    peers = [T.cores[r] for r in group if r != rank]

    g.sync.dma_start(T.stage[:], T.x[:]).then_inc(T.sem.staged, 16)
    g.sync.dma_start(mine, T.x[:]).then_inc(T.sem.arrived, 16)

    g.wait_ge(T.sem.staged, 16)
    ids = []
    for p in peers:
        rid, pid, _se = topo.addr(p)
        ids.append(DstId(rid=rid, pnc=pid))
    g.remote_dma_fused(
        [RemoteDMATransfer(dst_ids=ids, dma_engine_mask=0xFFFF, remote_sem=T.sem.arrived,
                           srcs=[T.stage[:]], dsts=[mine for _p in peers], alu_op=0)],
        local_sem=T.sem.sent)

    g.sync.wait_ge(T.sem.arrived, 16 * (len(peers) + 1))
    g.sync.dma_start(T.y[:], T.land[:]).then_inc(T.sem.stored, 16)
    g.wait_ge(T.sem.sent, 16)
    g.sync.wait_ge(T.sem.stored, 16)
